import numpy as np
import ml_dtypes


def mxq(x, axis, fmt="e4m3"):
    dtype, down = {"e4m3": (ml_dtypes.float8_e4m3fn, 7), "e5m2": (ml_dtypes.float8_e5m2, 14)}[fmt]
    v = np.moveaxis(np.asarray(x, np.float32).astype(ml_dtypes.bfloat16).astype(np.float64), axis, -1)
    blocks = v.reshape(v.shape[:-1] + (-1, 32))
    amax = np.abs(blocks).max(-1, keepdims=True)
    byte = np.maximum(np.where(amax > 0, np.frexp(amax)[1] - 1 + 127, 0) - down, 1)
    scale = np.exp2(byte - 127.0)
    codes = (blocks / scale).astype(np.float32).astype(dtype).astype(np.float64)
    return np.moveaxis((codes * scale).reshape(v.shape), -1, axis)


WIDE = False


def mx_kscale(k, group=512):
    if not WIDE:
        return np.ones(k)
    levels = np.array([18, -18])
    if group != 512:
        return np.exp2(np.random.permutation(np.resize(levels, k // group))).repeat(group)
    if k % 512:
        return np.exp2(np.random.permutation(np.resize(levels, k // 32))).repeat(32)
    a = np.empty((k // 512, 16))
    for p in range(k // 512):
        a[p, :8] = np.random.permutation(np.resize(levels, 8))
        for g in range(8):
            far = levels[np.abs(levels - a[p, g]) >= 10]
            a[p, g + 8] = far[np.random.randint(len(far))]
    return np.exp2(a.ravel()).repeat(32)


def f64(x):
    return np.asarray(x).astype(np.float64)


def sigmoid(v):
    return 1.0 / (1.0 + np.exp(-v))


G, D, M, N = 4, 128, 128, 512


def setup_inputs():
    n = np.random.standard_normal
    s_d = mx_kscale(D, 0)
    return {
        "x": (n((G, D, N)) * s_d[:, None]).astype(np.float32),
        "w1": (n((G, D, M)) / np.sqrt(D) / s_d[:, None]).astype(np.float32),
        "w2": (n((G, D, M)) / np.sqrt(D) / s_d[:, None]).astype(np.float32),
        "st": (np.random.uniform(4.0, 16.0, (G, M, 1))).astype(np.float32),
        "gb": (0.5 * n((G, M, 1))).astype(np.float32),
        "dx": (n((G, D, N)) * s_d[:, None]).astype(np.float32),
        "og": (np.random.uniform(0.5, 2.0, (G, M, 1))).astype(np.float32),
        "base": (0.3 * n((G, M, N))).astype(np.float32),
    }


def reference(x, w1, w2, st, gb, dx, og, base):
    w1q = mxq(f64(w1), 1, "e4m3")
    xq = mxq(f64(x), 1, "e4m3")
    z1 = w1q.transpose(0, 2, 1) @ xq
    dxq = mxq(f64(dx), 1, "e4m3")
    tz1 = w1q.transpose(0, 2, 1) @ dxq
    w2q = mxq(f64(w2), 1, "e4m3")
    z2 = w2q.transpose(0, 2, 1) @ xq
    tz2 = w2q.transpose(0, 2, 1) @ dxq
    mu = np.mean(z1 * z2, axis=-1, keepdims=True)
    gt = sigmoid(mu * f64(st) + f64(gb))
    xmu = np.mean(tz1 * z2 + tz2 * z1, axis=-1, keepdims=True)
    xgt = xmu * f64(st) * gt * (1.0 - gt)
    xh = tz1 * gt + xgt * z1
    y = xh * f64(og) + f64(base)
    return y

@@ -1,0 +1,225 @@
+from contextlib import ExitStack
+
+import concourse.mybir as mybir
+
+G, D, M, N = 4, 128, 128, 512
+FLOPS = 4 * 2 * G * D * M * N
+
+F32 = mybir.dt.float32
+BF16 = mybir.dt.bfloat16
+U32 = mybir.dt.uint32
+U8 = mybir.dt.uint8
+FP8X4 = mybir.dt.float8_e4m3fn_x4
+ALU = mybir.AluOpType
+ACT = mybir.ActivationFunctionType
+
+P = 128
+PACK = 4
+ROWS = D // PACK
+HALF = N // 2
+X_VECTOR_COLS = 352
+OFFLOADED = (0,)
+
+
+def tile_rows_tnrowgate_kernel(tc, x, w1, w2, st, gb, dx, og, base, out):
+    nc = tc.nc
+
+    with ExitStack() as ctx:
+        sb = ctx.enter_context(tc.tile_pool(name="sb", bufs=1))
+        ps = ctx.enter_context(tc.psum_pool(name="ps", bufs=1))
+        ctx.enter_context(tc.manual_schedule())
+
+        def tile(name, shape, dtype):
+            return sb.tile(shape, dtype, name=name, align_bytes=64)
+
+        def columns(name):
+            return [tile("%s%d" % (name, g), [P, 1], F32) for g in range(G)]
+
+        def planes(name):
+            return [tile("%s%d" % (name, g), [P, N], F32) for g in range(G)]
+
+        def load_rows(name, src):
+            raw = tile(name, [P, PACK, src.shape[2]], F32)
+            nc.sync.dma_start(out=raw[:], in_=src.rearrange("g (p j) n -> (g p) j n", j=PACK))
+            return raw
+
+        def views(packed, raw, first, last):
+            dst = packed[:, PACK * first : PACK * last].rearrange("p (c i j) -> p c j i", i=4, j=PACK)
+            src = raw[:, :, first:last].rearrange("p j (c i) -> p c j i", i=4)
+            return dst, src
+
+        def quantize(codes, scales, packed, first, last):
+            nc.vector.quantize_mx(
+                out=codes[:, first:last].bitcast(FP8X4),
+                scales=scales[:, first:last],
+                in_=packed[:, PACK * first : PACK * last],
+            )
+
+        def operand(name, width):
+            return (
+                tile(name + "_packed", [P, PACK * width], BF16),
+                tile(name + "_codes", [P, width], U32),
+                tile(name + "_scales", [P, width], U8),
+            )
+
+        def product(bank, g, weights, inputs):
+            rows = slice(ROWS * g, ROWS * (g + 1))
+            nc.tensor.matmul_mx(
+                out=bank[:],
+                lhsT=weights[1][rows, :].bitcast(FP8X4),
+                lhsT_scale=weights[2][rows, :],
+                rhs=inputs[1][rows, :].bitcast(FP8X4),
+                rhs_scale=inputs[2][rows, :],
+                start=True,
+                stop=True,
+            )
+
+        bank_a = [ps.tile([P, N], F32, name="bank_a%d" % g) for g in range(G)]
+        bank_b = [ps.tile([P, N], F32, name="bank_b%d" % g) for g in range(G)]
+
+        vec_rows = tile("vec_rows", [P, M], F32)
+        nc.gpsimd.memset(vec_rows[:], 0.0)
+        warm = tile("warm", [P, 1], F32)
+        warm_in = tile("warm_in", [P, 1], F32)
+        nc.gpsimd.memset(warm_in[:], 0.0)
+        nc.scalar.activation(out=warm[:], in_=warm_in[:], func=ACT.Sigmoid)
+        x_raw = load_rows("x_raw", x)
+        for r, vec in enumerate((st, gb, og)):
+            nc.sync.dma_start(
+                out=vec_rows[r:P:32, :].rearrange("b (g c) -> b g c", g=G),
+                in_=vec.rearrange("g (b c) o -> b g (c o)", c=32),
+            )
+        w1_raw = load_rows("w1_raw", w1)
+        w2_raw = load_rows("w2_raw", w2)
+        dx_raw = load_rows("dx_raw", dx)
+        base_sb = tile("base_sb", [P, G, N], F32)
+        nc.sync.dma_start(out=base_sb[:], in_=base.rearrange("g m n -> m g n"))
+
+
+        xq, dxq = operand("x", N), operand("dx", N)
+        w1q, w2q = operand("w1", M), operand("w2", M)
+        nc.vector.tensor_copy(*views(xq[0], x_raw, 0, HALF))
+        nc.vector.tensor_copy(*views(xq[0], x_raw, HALF, X_VECTOR_COLS))
+        nc.scalar.copy(*views(xq[0], x_raw, X_VECTOR_COLS, N))
+        nc.scalar.copy(*views(w1q[0], w1_raw, 0, M))
+        nc.scalar.copy(*views(w2q[0], w2_raw, 0, M))
+        quantize(xq[1], xq[2], xq[0], 0, HALF)
+        quantize(xq[1], xq[2], xq[0], HALF, N)
+        quantize(w1q[1], w1q[2], w1q[0], 0, M)
+        for g in range(G):
+            product(bank_a[g], g, w1q, xq)
+        quantize(w2q[1], w2q[2], w2q[0], 0, M)
+        for g in range(G):
+            product(bank_b[g], g, w2q, xq)
+
+        vecs = tile("vecs", [P, M], F32)
+        nc.vector.transpose(vecs[:], vec_rows[:])
+        st_n = tile("st_n", [P, G], F32)
+        neg_st_n = tile("neg_st_n", [P, G], F32)
+        nc.vector.tensor_scalar(out=st_n[:], in0=vecs[:, 0:M:32], scalar1=1.0 / N, scalar2=None, op0=ALU.mult)
+        nc.vector.tensor_scalar(out=neg_st_n[:], in0=vecs[:, 0:M:32], scalar1=-1.0 / N, scalar2=None, op0=ALU.mult)
+
+        z1 = planes("z1_")
+        u = planes("u")
+        ub = planes("ub")
+        v = planes("v")
+        y = planes("y")
+        junk_c, junk_d, junk_e = planes("jc"), planes("jd"), planes("je")
+        mu, gt, a, c, b, sum_d, sum_e = (columns(n) for n in ("mu", "gt", "a", "c", "b", "sum_d", "sum_e"))
+
+        def copy_z1(g):
+            nc.scalar.copy(z1[g][:], bank_a[g][:])
+
+        def row_sum(junk, bank, factor, other, total):
+            nc.vector.scalar_tensor_tensor(
+                out=junk[:], in0=bank[:], scalar=factor, in1=other[:], op0=ALU.mult, op1=ALU.mult, accum_out=total[:]
+            )
+
+        def sum_c(g):
+            row_sum(junk_c[g], bank_b[g], 1.0, z1[g], mu[g])
+
+        def gate(g):
+            col = slice(g, g + 1)
+            nc.scalar.activation(
+                out=gt[g][:], in_=mu[g][:], func=ACT.Sigmoid, scale=st_n[:, col], bias=vecs[:, 32 * g + 1 : 32 * g + 2]
+            )
+
+        def factors(g):
+            col = slice(g, g + 1)
+            nc.scalar.activation(out=a[g][:], in_=gt[g][:], func=ACT.Copy, scale=vecs[:, 32 * g + 2 : 32 * g + 3])
+            nc.scalar.activation(
+                out=c[g][:], in_=gt[g][:], func=ACT.Identity, scale=neg_st_n[:, col], bias=st_n[:, col]
+            )
+
+        def scale_tz1(g):
+            nc.scalar.activation(out=u[g][:], in_=bank_a[g][:], func=ACT.Copy, scale=a[g][:])
+            product(bank_a[g], g, w2q, dxq)
+
+        def add_base(g):
+            nc.gpsimd.tensor_tensor(out=ub[g][:], in0=u[g][:], in1=base_sb[:, g, :], op=ALU.add)
+
+        def sum_d_of(g):
+            row_sum(junk_d[g], bank_b[g], c[g][:], u[g], sum_d[g])
+            if g not in OFFLOADED:
+                product(bank_b[g], g, w1q, xq)
+
+        def sum_e_of(g):
+            row_sum(junk_e[g], bank_a[g], a[g][:], z1[g], sum_e[g])
+            nc.scalar.activation(
+                out=b[g][:], in_=sum_e[g][:], func=ACT.Identity, scale=c[g][:], bias=sum_d[g][:]
+            )
+            if g in OFFLOADED:
+                nc.scalar.activation(out=v[g][:], in_=z1[g][:], func=ACT.Copy, scale=b[g][:])
+
+        def finish(g):
+            if g in OFFLOADED:
+                nc.gpsimd.tensor_tensor(out=y[g][:], in0=v[g][:], in1=ub[g][:], op=ALU.add)
+            else:
+                nc.vector.scalar_tensor_tensor(
+                    out=y[g][:], in0=bank_b[g][:], scalar=b[g][:], in1=ub[g][:], op0=ALU.mult, op1=ALU.add
+                )
+            nc.sync.dma_start(out=out[g], in_=y[g][:])
+
+        copy_z1(0)
+        copy_z1(1)
+        dst, src = views(dxq[0], dx_raw, 0, HALF)
+        nc.gpsimd.tensor_scalar(out=dst, in0=src, scalar1=1.0, scalar2=0.0, op0=ALU.mult, op1=ALU.add)
+        nc.scalar.copy(*views(dxq[0], dx_raw, HALF, N))
+        sum_c(0)
+        sum_c(1)
+        quantize(dxq[1], dxq[2], dxq[0], 0, HALF)
+        quantize(dxq[1], dxq[2], dxq[0], HALF, N)
+        copy_z1(2)
+        copy_z1(3)
+        for g in range(G):
+            product(bank_a[g], g, w1q, dxq)
+        sum_c(2)
+        sum_c(3)
+        gate(0)
+        gate(1)
+        factors(0)
+        factors(1)
+        scale_tz1(0)
+        add_base(0)
+        scale_tz1(1)
+        add_base(1)
+        sum_d_of(0)
+        sum_d_of(1)
+        gate(2)
+        gate(3)
+        factors(2)
+        factors(3)
+        scale_tz1(2)
+        add_base(2)
+        scale_tz1(3)
+        sum_e_of(0)
+        sum_d_of(2)
+        sum_e_of(1)
+        sum_d_of(3)
+        finish(0)
+        add_base(3)
+        sum_e_of(2)
+        finish(1)
+        sum_e_of(3)
+        finish(2)
+        finish(3)

@@ -16,9 +16,16 @@ ACT = mybir.ActivationFunctionType
 P = 128
 PACK = 4
 ROWS = D // PACK
+PAIR = 2
+RUN = 4
+BLOCK = 32
 HALF = N // 2
+LAST = G - 1
+
 X_VECTOR_COLS = 352
-OFFLOADED = (0,)
+POOL_FACTOR_GROUPS = 2
+FIRST_VECTOR_COLS = 256
+FINISH_LAG = 3
 
 
 def tile_rows_tnrowgate_kernel(tc, x, w1, w2, st, gb, dx, og, base, out):
@@ -32,44 +39,43 @@ def tile_rows_tnrowgate_kernel(tc, x, w1, w2, st, gb, dx, og, base, out):
         def tile(name, shape, dtype):
             return sb.tile(shape, dtype, name=name, align_bytes=64)
 
-        def columns(name):
-            return [tile("%s%d" % (name, g), [P, 1], F32) for g in range(G)]
+        def per_group(name, width):
+            return [tile("%s%d" % (name, g), [P, width], F32) for g in range(G)]
 
-        def planes(name):
-            return [tile("%s%d" % (name, g), [P, N], F32) for g in range(G)]
-
-        def load_rows(name, src):
-            raw = tile(name, [P, PACK, src.shape[2]], F32)
-            nc.sync.dma_start(out=raw[:], in_=src.rearrange("g (p j) n -> (g p) j n", j=PACK))
+        def load_rows(name, src, first, count):
+            raw = tile(name, [P, count, src.shape[2]], F32)
+            rows = src.rearrange("g (p j) n -> (g p) j n", j=PACK)
+            nc.sync.dma_start(out=raw[:], in_=rows[:, first : first + count, :])
             return raw
 
-        def views(packed, raw, first, last):
-            dst = packed[:, PACK * first : PACK * last].rearrange("p (c i j) -> p c j i", i=4, j=PACK)
-            src = raw[:, :, first:last].rearrange("p j (c i) -> p c j i", i=4)
-            return dst, src
-
-        def quantize(codes, scales, packed, first, last):
-            nc.vector.quantize_mx(
-                out=codes[:, first:last].bitcast(FP8X4),
-                scales=scales[:, first:last],
-                in_=packed[:, PACK * first : PACK * last],
-            )
-
         def operand(name, width):
-            return (
-                tile(name + "_packed", [P, PACK * width], BF16),
-                tile(name + "_codes", [P, width], U32),
-                tile(name + "_scales", [P, width], U8),
+            return {
+                "packed": tile(name + "_packed", [P, PACK * width], BF16),
+                "codes": tile(name + "_codes", [P, width], U32),
+                "scales": tile(name + "_scales", [P, width], U8),
+            }
+
+        def pack(copy, target, raw, first_row, cols):
+            dst = target["packed"][:, PACK * cols.start : PACK * cols.stop]
+            dst = dst.rearrange("p (c i j) -> p c j i", i=RUN, j=PACK)
+            src = raw[:, :, cols].rearrange("p j (c i) -> p c j i", i=RUN)
+            copy(dst[:, :, first_row : first_row + raw.shape[1], :], src)
+
+        def quantize(target, cols):
+            nc.vector.quantize_mx(
+                out=target["codes"][:, cols].bitcast(FP8X4),
+                scales=target["scales"][:, cols],
+                in_=target["packed"][:, PACK * cols.start : PACK * cols.stop],
             )
 
         def product(bank, g, weights, inputs):
             rows = slice(ROWS * g, ROWS * (g + 1))
             nc.tensor.matmul_mx(
                 out=bank[:],
-                lhsT=weights[1][rows, :].bitcast(FP8X4),
-                lhsT_scale=weights[2][rows, :],
-                rhs=inputs[1][rows, :].bitcast(FP8X4),
-                rhs_scale=inputs[2][rows, :],
+                lhsT=weights["codes"][rows, :].bitcast(FP8X4),
+                lhsT_scale=weights["scales"][rows, :],
+                rhs=inputs["codes"][rows, :].bitcast(FP8X4),
+                rhs_scale=inputs["scales"][rows, :],
                 start=True,
                 stop=True,
             )
@@ -79,147 +85,151 @@ def tile_rows_tnrowgate_kernel(tc, x, w1, w2, st, gb, dx, og, base, out):
 
         vec_rows = tile("vec_rows", [P, M], F32)
         nc.gpsimd.memset(vec_rows[:], 0.0)
-        warm = tile("warm", [P, 1], F32)
+
         warm_in = tile("warm_in", [P, 1], F32)
+        warm_out = tile("warm_out", [P, 1], F32)
         nc.gpsimd.memset(warm_in[:], 0.0)
-        nc.scalar.activation(out=warm[:], in_=warm_in[:], func=ACT.Sigmoid)
-        x_raw = load_rows("x_raw", x)
+        nc.scalar.activation(out=warm_out[:], in_=warm_in[:], func=ACT.Sigmoid)
+
+        x_raw = [load_rows("x_raw%d" % j, x, j, PAIR) for j in (0, PAIR)]
         for r, vec in enumerate((st, gb, og)):
             nc.sync.dma_start(
-                out=vec_rows[r:P:32, :].rearrange("b (g c) -> b g c", g=G),
-                in_=vec.rearrange("g (b c) o -> b g (c o)", c=32),
+                out=vec_rows[r:P:BLOCK, :].rearrange("q (g i) -> q g i", g=G),
+                in_=vec.rearrange("g (q i) o -> q g (i o)", i=BLOCK),
             )
-        w1_raw = load_rows("w1_raw", w1)
-        w2_raw = load_rows("w2_raw", w2)
-        dx_raw = load_rows("dx_raw", dx)
+        w1_raw = load_rows("w1_raw", w1, 0, PACK)
+        w2_raw = load_rows("w2_raw", w2, 0, PACK)
+        dx_raw = [load_rows("dx_raw%d" % j, dx, j, PAIR) for j in (0, PAIR)]
         base_sb = tile("base_sb", [P, G, N], F32)
         nc.sync.dma_start(out=base_sb[:], in_=base.rearrange("g m n -> m g n"))
 
-
         xq, dxq = operand("x", N), operand("dx", N)
         w1q, w2q = operand("w1", M), operand("w2", M)
-        nc.vector.tensor_copy(*views(xq[0], x_raw, 0, HALF))
-        nc.vector.tensor_copy(*views(xq[0], x_raw, HALF, X_VECTOR_COLS))
-        nc.scalar.copy(*views(xq[0], x_raw, X_VECTOR_COLS, N))
-        nc.scalar.copy(*views(w1q[0], w1_raw, 0, M))
-        nc.scalar.copy(*views(w2q[0], w2_raw, 0, M))
-        quantize(xq[1], xq[2], xq[0], 0, HALF)
-        quantize(xq[1], xq[2], xq[0], HALF, N)
-        quantize(w1q[1], w1q[2], w1q[0], 0, M)
-        for g in range(G):
-            product(bank_a[g], g, w1q, xq)
-        quantize(w2q[1], w2q[2], w2q[0], 0, M)
-        for g in range(G):
-            product(bank_b[g], g, w2q, xq)
+        all_n, all_m = slice(0, N), slice(0, M)
+        low_n, high_n = slice(0, HALF), slice(HALF, N)
 
+        pack(nc.vector.tensor_copy, xq, x_raw[0], 0, all_n)
+        pack(nc.vector.tensor_copy, xq, x_raw[1], PAIR, low_n)
+        pack(nc.vector.tensor_copy, xq, x_raw[1], PAIR, slice(HALF, X_VECTOR_COLS))
+        pack(nc.scalar.copy, xq, x_raw[1], PAIR, slice(X_VECTOR_COLS, N))
+        pack(nc.scalar.copy, w1q, w1_raw, 0, all_m)
+        pack(nc.scalar.copy, w2q, w2_raw, 0, all_m)
+        quantize(xq, low_n)
+        quantize(xq, high_n)
+        for weights, banks in ((w1q, bank_a), (w2q, bank_b)):
+            quantize(weights, all_m)
+            for g in range(G):
+                product(banks[g], g, weights, xq)
+
+        z1, u, u_base, y = (per_group(name, N) for name in ("z1_", "u", "u_base", "y"))
+        terms_mu, terms_u, terms_t = (per_group(name, N) for name in ("terms_mu", "terms_u", "terms_t"))
+        sum_mu, sum_u, sum_t = (per_group(name, 1) for name in ("sum_mu", "sum_u", "sum_t"))
+        gt, a, b, c = (per_group(name, 1) for name in ("gt", "a", "b", "c"))
         vecs = tile("vecs", [P, M], F32)
-        nc.vector.transpose(vecs[:], vec_rows[:])
         st_n = tile("st_n", [P, G], F32)
         neg_st_n = tile("neg_st_n", [P, G], F32)
-        nc.vector.tensor_scalar(out=st_n[:], in0=vecs[:, 0:M:32], scalar1=1.0 / N, scalar2=None, op0=ALU.mult)
-        nc.vector.tensor_scalar(out=neg_st_n[:], in0=vecs[:, 0:M:32], scalar1=-1.0 / N, scalar2=None, op0=ALU.mult)
 
-        z1 = planes("z1_")
-        u = planes("u")
-        ub = planes("ub")
-        v = planes("v")
-        y = planes("y")
-        junk_c, junk_d, junk_e = planes("jc"), planes("jd"), planes("je")
-        mu, gt, a, c, b, sum_d, sum_e = (columns(n) for n in ("mu", "gt", "a", "c", "b", "sum_d", "sum_e"))
+        def column(source, index):
+            return source[:, index : index + 1]
 
-        def copy_z1(g):
-            nc.scalar.copy(z1[g][:], bank_a[g][:])
+        def pool_affine(target, source, factor, term):
+            nc.gpsimd.tensor_scalar(out=target, in0=source, scalar1=factor, scalar2=term, op0=ALU.mult, op1=ALU.add)
 
-        def row_sum(junk, bank, factor, other, total):
+        def row_sum(terms, bank, factor, other, total):
             nc.vector.scalar_tensor_tensor(
-                out=junk[:], in0=bank[:], scalar=factor, in1=other[:], op0=ALU.mult, op1=ALU.mult, accum_out=total[:]
+                out=terms[:], in0=bank[:], scalar=factor, in1=other[:], op0=ALU.mult, op1=ALU.mult, accum_out=total[:]
             )
 
-        def sum_c(g):
-            row_sum(junk_c[g], bank_b[g], 1.0, z1[g], mu[g])
+        def keep_z1(g):
+            nc.scalar.copy(z1[g][:], bank_a[g][:])
 
         def gate(g):
-            col = slice(g, g + 1)
             nc.scalar.activation(
-                out=gt[g][:], in_=mu[g][:], func=ACT.Sigmoid, scale=st_n[:, col], bias=vecs[:, 32 * g + 1 : 32 * g + 2]
+                out=gt[g][:], in_=sum_mu[g][:], func=ACT.Sigmoid, scale=column(st_n, g), bias=column(vecs, BLOCK * g + 1)
             )
 
         def factors(g):
-            col = slice(g, g + 1)
-            nc.scalar.activation(out=a[g][:], in_=gt[g][:], func=ACT.Copy, scale=vecs[:, 32 * g + 2 : 32 * g + 3])
-            nc.scalar.activation(
-                out=c[g][:], in_=gt[g][:], func=ACT.Identity, scale=neg_st_n[:, col], bias=st_n[:, col]
-            )
-
-        def scale_tz1(g):
-            nc.scalar.activation(out=u[g][:], in_=bank_a[g][:], func=ACT.Copy, scale=a[g][:])
-            product(bank_a[g], g, w2q, dxq)
+            gain = column(vecs, BLOCK * g + 2)
+            if g < POOL_FACTOR_GROUPS:
+                pool_affine(a[g][:], gt[g][:], gain, 0.0)
+                pool_affine(c[g][:], gt[g][:], column(neg_st_n, g), column(st_n, g))
+            else:
+                nc.scalar.activation(out=a[g][:], in_=gt[g][:], func=ACT.Copy, scale=gain)
+                nc.scalar.activation(
+                    out=c[g][:], in_=gt[g][:], func=ACT.Identity, scale=column(neg_st_n, g), bias=column(st_n, g)
+                )
 
         def add_base(g):
-            nc.gpsimd.tensor_tensor(out=ub[g][:], in0=u[g][:], in1=base_sb[:, g, :], op=ALU.add)
+            nc.gpsimd.tensor_tensor(out=u_base[g][:], in0=u[g][:], in1=base_sb[:, g, :], op=ALU.add)
 
-        def sum_d_of(g):
-            row_sum(junk_d[g], bank_b[g], c[g][:], u[g], sum_d[g])
-            if g not in OFFLOADED:
-                product(bank_b[g], g, w1q, xq)
-
-        def sum_e_of(g):
-            row_sum(junk_e[g], bank_a[g], a[g][:], z1[g], sum_e[g])
-            nc.scalar.activation(
-                out=b[g][:], in_=sum_e[g][:], func=ACT.Identity, scale=c[g][:], bias=sum_d[g][:]
+        def finish(g, cols):
+            nc.vector.scalar_tensor_tensor(
+                out=y[g][:, cols],
+                in0=bank_b[g][:, cols],
+                scalar=b[g][:],
+                in1=u_base[g][:, cols],
+                op0=ALU.mult,
+                op1=ALU.add,
             )
-            if g in OFFLOADED:
-                nc.scalar.activation(out=v[g][:], in_=z1[g][:], func=ACT.Copy, scale=b[g][:])
 
-        def finish(g):
-            if g in OFFLOADED:
-                nc.gpsimd.tensor_tensor(out=y[g][:], in0=v[g][:], in1=ub[g][:], op=ALU.add)
-            else:
-                nc.vector.scalar_tensor_tensor(
-                    out=y[g][:], in0=bank_b[g][:], scalar=b[g][:], in1=ub[g][:], op0=ALU.mult, op1=ALU.add
-                )
-            nc.sync.dma_start(out=out[g], in_=y[g][:])
+        def finish_off_vector(g, cols):
+            scaled = tile("b_z1", [P, cols.stop - cols.start], F32)
+            nc.scalar.activation(out=scaled[:], in_=z1[g][:, cols], func=ACT.Copy, scale=b[g][:])
+            nc.gpsimd.tensor_tensor(out=y[g][:, cols], in0=scaled[:], in1=u_base[g][:, cols], op=ALU.add)
 
-        copy_z1(0)
-        copy_z1(1)
-        dst, src = views(dxq[0], dx_raw, 0, HALF)
-        nc.gpsimd.tensor_scalar(out=dst, in0=src, scalar1=1.0, scalar2=0.0, op0=ALU.mult, op1=ALU.add)
-        nc.scalar.copy(*views(dxq[0], dx_raw, HALF, N))
-        sum_c(0)
-        sum_c(1)
-        quantize(dxq[1], dxq[2], dxq[0], 0, HALF)
-        quantize(dxq[1], dxq[2], dxq[0], HALF, N)
-        copy_z1(2)
-        copy_z1(3)
+        def store(g, cols):
+            nc.sync.dma_start(out=out[g][:, cols], in_=y[g][:, cols])
+
+        pack(nc.vector.tensor_copy, dxq, dx_raw[0], 0, all_n)
+        nc.vector.transpose(vecs[:], vec_rows[:])
+        pool_affine(st_n[:], vecs[:, 0:M:BLOCK], 1.0 / N, 0.0)
+        pool_affine(neg_st_n[:], vecs[:, 0:M:BLOCK], -1.0 / N, 0.0)
+        keep_z1(0)
+        pack(nc.vector.tensor_copy, dxq, dx_raw[1], PAIR, low_n)
+        pack(nc.scalar.copy, dxq, dx_raw[1], PAIR, high_n)
+        row_sum(terms_mu[0], bank_b[0], 1.0, z1[0], sum_mu[0])
+        quantize(dxq, all_n)
+
+        keep_z1(1)
+        for g in range(POOL_FACTOR_GROUPS):
+            keep_z1(g + 2)
+            gate(g)
+            factors(g)
+            row_sum(terms_mu[g + 1], bank_b[g + 1], 1.0, z1[g + 1], sum_mu[g + 1])
+        row_sum(terms_mu[LAST], bank_b[LAST], 1.0, z1[LAST], sum_mu[LAST])
         for g in range(G):
             product(bank_a[g], g, w1q, dxq)
-        sum_c(2)
-        sum_c(3)
-        gate(0)
-        gate(1)
-        factors(0)
-        factors(1)
-        scale_tz1(0)
-        add_base(0)
-        scale_tz1(1)
-        add_base(1)
-        sum_d_of(0)
-        sum_d_of(1)
-        gate(2)
-        gate(3)
-        factors(2)
-        factors(3)
-        scale_tz1(2)
-        add_base(2)
-        scale_tz1(3)
-        sum_e_of(0)
-        sum_d_of(2)
-        sum_e_of(1)
-        sum_d_of(3)
-        finish(0)
-        add_base(3)
-        sum_e_of(2)
-        finish(1)
-        sum_e_of(3)
-        finish(2)
-        finish(3)
+
+        for step in range(G + FINISH_LAG):
+            if step < G:
+                g = step
+                nc.scalar.activation(out=u[g][:], in_=bank_a[g][:], func=ACT.Copy, scale=a[g][:])
+                product(bank_a[g], g, w2q, dxq)
+                if g < LAST:
+                    add_base(g)
+                if POOL_FACTOR_GROUPS <= g + 1 < G:
+                    factors(g + 1)
+                if g + 2 < G:
+                    gate(g + 2)
+            if step >= FINISH_LAG:
+                g = step - FINISH_LAG
+                nc.scalar.activation(
+                    out=b[g][:], in_=sum_t[g][:], func=ACT.Identity, scale=c[g][:], bias=sum_u[g][:]
+                )
+                if g == 0:
+                    finish_off_vector(g, slice(FIRST_VECTOR_COLS, N))
+                    add_base(LAST)
+                if g == LAST:
+                    for cols in (low_n, high_n):
+                        finish(g, cols)
+                        store(g, cols)
+                else:
+                    finish(g, slice(0, FIRST_VECTOR_COLS) if g == 0 else all_n)
+                    store(g, all_n)
+            if step < G:
+                g = step
+                row_sum(terms_u[g], bank_b[g], c[g][:], u[g], sum_u[g])
+                product(bank_b[g], g, w1q, xq)
+            if 1 <= step <= G:
+                g = step - 1
+                row_sum(terms_t[g], bank_a[g], a[g][:], z1[g], sum_t[g])

@@ -24,7 +24,6 @@ LAST = G - 1
 
 X_VECTOR_COLS = 352
 POOL_FACTOR_GROUPS = 2
-FIRST_VECTOR_COLS = 256
 FINISH_LAG = 3
 
 
@@ -86,19 +85,14 @@ def tile_rows_tnrowgate_kernel(tc, x, w1, w2, st, gb, dx, og, base, out):
         vec_rows = tile("vec_rows", [P, M], F32)
         nc.gpsimd.memset(vec_rows[:], 0.0)
 
-        warm_in = tile("warm_in", [P, 1], F32)
-        warm_out = tile("warm_out", [P, 1], F32)
-        nc.gpsimd.memset(warm_in[:], 0.0)
-        nc.scalar.activation(out=warm_out[:], in_=warm_in[:], func=ACT.Sigmoid)
-
         x_raw = [load_rows("x_raw%d" % j, x, j, PAIR) for j in (0, PAIR)]
+        w1_raw = load_rows("w1_raw", w1, 0, PACK)
+        w2_raw = load_rows("w2_raw", w2, 0, PACK)
         for r, vec in enumerate((st, gb, og)):
             nc.sync.dma_start(
                 out=vec_rows[r:P:BLOCK, :].rearrange("q (g i) -> q g i", g=G),
                 in_=vec.rearrange("g (q i) o -> q g (i o)", i=BLOCK),
             )
-        w1_raw = load_rows("w1_raw", w1, 0, PACK)
-        w2_raw = load_rows("w2_raw", w2, 0, PACK)
         dx_raw = [load_rows("dx_raw%d" % j, dx, j, PAIR) for j in (0, PAIR)]
         base_sb = tile("base_sb", [P, G, N], F32)
         nc.sync.dma_start(out=base_sb[:], in_=base.rearrange("g m n -> m g n"))
@@ -116,18 +110,22 @@ def tile_rows_tnrowgate_kernel(tc, x, w1, w2, st, gb, dx, og, base, out):
         pack(nc.scalar.copy, w2q, w2_raw, 0, all_m)
         quantize(xq, low_n)
         quantize(xq, high_n)
-        for weights, banks in ((w1q, bank_a), (w2q, bank_b)):
-            quantize(weights, all_m)
-            for g in range(G):
-                product(banks[g], g, weights, xq)
+        quantize(w1q, all_m)
+        product(bank_a[0], 0, w1q, xq)
+        quantize(w2q, all_m)
+        for g in range(G):
+            if g < LAST:
+                product(bank_a[g + 1], g + 1, w1q, xq)
+            product(bank_b[g], g, w2q, xq)
 
         z1, u, u_base, y = (per_group(name, N) for name in ("z1_", "u", "u_base", "y"))
         terms_mu, terms_u, terms_t = (per_group(name, N) for name in ("terms_mu", "terms_u", "terms_t"))
         sum_mu, sum_u, sum_t = (per_group(name, 1) for name in ("sum_mu", "sum_u", "sum_t"))
-        gt, a, b, c = (per_group(name, 1) for name in ("gt", "a", "b", "c"))
+        th, a, b, c = (per_group(name, 1) for name in ("th", "a", "b", "c"))
         vecs = tile("vecs", [P, M], F32)
-        st_n = tile("st_n", [P, G], F32)
-        neg_st_n = tile("neg_st_n", [P, G], F32)
+        slope = tile("slope", [P, G], F32)
+        neg_slope = tile("neg_slope", [P, G], F32)
+        halves = tile("halves", [P, G, 2], F32)
 
         def column(source, index):
             return source[:, index : index + 1]
@@ -145,45 +143,45 @@ def tile_rows_tnrowgate_kernel(tc, x, w1, w2, st, gb, dx, og, base, out):
 
         def gate(g):
             nc.scalar.activation(
-                out=gt[g][:], in_=sum_mu[g][:], func=ACT.Sigmoid, scale=column(st_n, g), bias=column(vecs, BLOCK * g + 1)
+                out=th[g][:], in_=sum_mu[g][:], func=ACT.Tanh, scale=column(slope, g), bias=halves[:, g, 0:1]
             )
 
         def factors(g):
-            gain = column(vecs, BLOCK * g + 2)
-            if g < POOL_FACTOR_GROUPS:
-                pool_affine(a[g][:], gt[g][:], gain, 0.0)
-                pool_affine(c[g][:], gt[g][:], column(neg_st_n, g), column(st_n, g))
-            else:
-                nc.scalar.activation(out=a[g][:], in_=gt[g][:], func=ACT.Copy, scale=gain)
-                nc.scalar.activation(
-                    out=c[g][:], in_=gt[g][:], func=ACT.Identity, scale=column(neg_st_n, g), bias=column(st_n, g)
-                )
+            half_og = halves[:, g, 1:2]
+            for target, factor, term in ((a, half_og, half_og), (c, column(neg_slope, g), column(slope, g))):
+                if g < POOL_FACTOR_GROUPS:
+                    pool_affine(target[g][:], th[g][:], factor, term)
+                else:
+                    nc.scalar.activation(out=target[g][:], in_=th[g][:], func=ACT.Identity, scale=factor, bias=term)
 
         def add_base(g):
             nc.gpsimd.tensor_tensor(out=u_base[g][:], in0=u[g][:], in1=base_sb[:, g, :], op=ALU.add)
 
         def finish(g, cols):
+            z1_source = z1[g] if g == LAST else bank_b[g]
             nc.vector.scalar_tensor_tensor(
                 out=y[g][:, cols],
-                in0=bank_b[g][:, cols],
+                in0=z1_source[:, cols],
                 scalar=b[g][:],
                 in1=u_base[g][:, cols],
                 op0=ALU.mult,
                 op1=ALU.add,
             )
 
-        def finish_off_vector(g, cols):
-            scaled = tile("b_z1", [P, cols.stop - cols.start], F32)
-            nc.scalar.activation(out=scaled[:], in_=z1[g][:, cols], func=ACT.Copy, scale=b[g][:])
-            nc.gpsimd.tensor_tensor(out=y[g][:, cols], in0=scaled[:], in1=u_base[g][:, cols], op=ALU.add)
+        def finish_off_vector(g):
+            b_z1 = tile("b_z1", [P, N], F32)
+            nc.scalar.activation(out=b_z1[:], in_=z1[g][:], func=ACT.Copy, scale=b[g][:])
+            nc.gpsimd.tensor_tensor(out=y[g][:], in0=b_z1[:], in1=u_base[g][:], op=ALU.add)
 
         def store(g, cols):
             nc.sync.dma_start(out=out[g][:, cols], in_=y[g][:, cols])
 
         pack(nc.vector.tensor_copy, dxq, dx_raw[0], 0, all_n)
         nc.vector.transpose(vecs[:], vec_rows[:])
-        pool_affine(st_n[:], vecs[:, 0:M:BLOCK], 1.0 / N, 0.0)
-        pool_affine(neg_st_n[:], vecs[:, 0:M:BLOCK], -1.0 / N, 0.0)
+        by_group = vecs[:].rearrange("p (g r) -> p g r", g=G)
+        pool_affine(slope[:], by_group[:, :, 0], 0.5 / N, 0.0)
+        pool_affine(halves[:], by_group[:, :, 1:3], 0.5, 0.0)
+        pool_affine(neg_slope[:], by_group[:, :, 0], -0.5 / N, 0.0)
         keep_z1(0)
         pack(nc.vector.tensor_copy, dxq, dx_raw[1], PAIR, low_n)
         pack(nc.scalar.copy, dxq, dx_raw[1], PAIR, high_n)
@@ -217,19 +215,21 @@ def tile_rows_tnrowgate_kernel(tc, x, w1, w2, st, gb, dx, og, base, out):
                     out=b[g][:], in_=sum_t[g][:], func=ACT.Identity, scale=c[g][:], bias=sum_u[g][:]
                 )
                 if g == 0:
-                    finish_off_vector(g, slice(FIRST_VECTOR_COLS, N))
+                    finish_off_vector(g)
+                    store(g, all_n)
                     add_base(LAST)
-                if g == LAST:
+                elif g == LAST:
                     for cols in (low_n, high_n):
                         finish(g, cols)
                         store(g, cols)
                 else:
-                    finish(g, slice(0, FIRST_VECTOR_COLS) if g == 0 else all_n)
+                    finish(g, all_n)
                     store(g, all_n)
             if step < G:
                 g = step
                 row_sum(terms_u[g], bank_b[g], c[g][:], u[g], sum_u[g])
-                product(bank_b[g], g, w1q, xq)
+                if 0 < g < LAST:
+                    product(bank_b[g], g, w1q, xq)
             if 1 <= step <= G:
                 g = step - 1
                 row_sum(terms_t[g], bank_a[g], a[g][:], z1[g], sum_t[g])

from contextlib import ExitStack

import concourse.mybir as mybir

G, D, M, N = 4, 128, 128, 512
FLOPS = 4 * 2 * G * D * M * N

F32 = mybir.dt.float32
BF16 = mybir.dt.bfloat16
U32 = mybir.dt.uint32
U8 = mybir.dt.uint8
FP8X4 = mybir.dt.float8_e4m3fn_x4
ALU = mybir.AluOpType
ACT = mybir.ActivationFunctionType

P = 128
PACK = 4
ROWS = D // PACK
PAIR = 2
RUN = 4
BLOCK = 32
HALF = N // 2
LAST = G - 1

X_VECTOR_COLS = 352
POOL_FACTOR_GROUPS = 2
FINISH_LAG = 3


def tile_rows_tnrowgate_kernel(tc, x, w1, w2, st, gb, dx, og, base, out):
    nc = tc.nc

    with ExitStack() as ctx:
        sb = ctx.enter_context(tc.tile_pool(name="sb", bufs=1))
        ps = ctx.enter_context(tc.psum_pool(name="ps", bufs=1))
        ctx.enter_context(tc.manual_schedule())

        def tile(name, shape, dtype):
            return sb.tile(shape, dtype, name=name, align_bytes=64)

        def per_group(name, width):
            return [tile("%s%d" % (name, g), [P, width], F32) for g in range(G)]

        def load_rows(name, src, first, count):
            raw = tile(name, [P, count, src.shape[2]], F32)
            rows = src.rearrange("g (p j) n -> (g p) j n", j=PACK)
            nc.sync.dma_start(out=raw[:], in_=rows[:, first : first + count, :])
            return raw

        def operand(name, width):
            return {
                "packed": tile(name + "_packed", [P, PACK * width], BF16),
                "codes": tile(name + "_codes", [P, width], U32),
                "scales": tile(name + "_scales", [P, width], U8),
            }

        def pack(copy, target, raw, first_row, cols):
            dst = target["packed"][:, PACK * cols.start : PACK * cols.stop]
            dst = dst.rearrange("p (c i j) -> p c j i", i=RUN, j=PACK)
            src = raw[:, :, cols].rearrange("p j (c i) -> p c j i", i=RUN)
            copy(dst[:, :, first_row : first_row + raw.shape[1], :], src)

        def quantize(target, cols):
            nc.vector.quantize_mx(
                out=target["codes"][:, cols].bitcast(FP8X4),
                scales=target["scales"][:, cols],
                in_=target["packed"][:, PACK * cols.start : PACK * cols.stop],
            )

        def product(bank, g, weights, inputs):
            rows = slice(ROWS * g, ROWS * (g + 1))
            nc.tensor.matmul_mx(
                out=bank[:],
                lhsT=weights["codes"][rows, :].bitcast(FP8X4),
                lhsT_scale=weights["scales"][rows, :],
                rhs=inputs["codes"][rows, :].bitcast(FP8X4),
                rhs_scale=inputs["scales"][rows, :],
                start=True,
                stop=True,
            )

        bank_a = [ps.tile([P, N], F32, name="bank_a%d" % g) for g in range(G)]
        bank_b = [ps.tile([P, N], F32, name="bank_b%d" % g) for g in range(G)]

        vec_rows = tile("vec_rows", [P, M], F32)
        nc.gpsimd.memset(vec_rows[:], 0.0)

        x_raw = [load_rows("x_raw%d" % j, x, j, PAIR) for j in (0, PAIR)]
        w1_raw = load_rows("w1_raw", w1, 0, PACK)
        w2_raw = load_rows("w2_raw", w2, 0, PACK)
        for r, vec in enumerate((st, gb, og)):
            nc.sync.dma_start(
                out=vec_rows[r:P:BLOCK, :].rearrange("q (g i) -> q g i", g=G),
                in_=vec.rearrange("g (q i) o -> q g (i o)", i=BLOCK),
            )
        dx_raw = [load_rows("dx_raw%d" % j, dx, j, PAIR) for j in (0, PAIR)]
        base_sb = tile("base_sb", [P, G, N], F32)
        nc.sync.dma_start(out=base_sb[:], in_=base.rearrange("g m n -> m g n"))

        xq, dxq = operand("x", N), operand("dx", N)
        w1q, w2q = operand("w1", M), operand("w2", M)
        all_n, all_m = slice(0, N), slice(0, M)
        low_n, high_n = slice(0, HALF), slice(HALF, N)

        pack(nc.vector.tensor_copy, xq, x_raw[0], 0, all_n)
        pack(nc.vector.tensor_copy, xq, x_raw[1], PAIR, low_n)
        pack(nc.vector.tensor_copy, xq, x_raw[1], PAIR, slice(HALF, X_VECTOR_COLS))
        pack(nc.scalar.copy, xq, x_raw[1], PAIR, slice(X_VECTOR_COLS, N))
        pack(nc.scalar.copy, w1q, w1_raw, 0, all_m)
        pack(nc.scalar.copy, w2q, w2_raw, 0, all_m)
        quantize(xq, low_n)
        quantize(xq, high_n)
        quantize(w1q, all_m)
        product(bank_a[0], 0, w1q, xq)
        quantize(w2q, all_m)
        for g in range(G):
            if g < LAST:
                product(bank_a[g + 1], g + 1, w1q, xq)
            product(bank_b[g], g, w2q, xq)

        z1, u, u_base, y = (per_group(name, N) for name in ("z1_", "u", "u_base", "y"))
        terms_mu, terms_u, terms_t = (per_group(name, N) for name in ("terms_mu", "terms_u", "terms_t"))
        sum_mu, sum_u, sum_t = (per_group(name, 1) for name in ("sum_mu", "sum_u", "sum_t"))
        th, a, b, c = (per_group(name, 1) for name in ("th", "a", "b", "c"))
        vecs = tile("vecs", [P, M], F32)
        slope = tile("slope", [P, G], F32)
        neg_slope = tile("neg_slope", [P, G], F32)
        halves = tile("halves", [P, G, 2], F32)

        def column(source, index):
            return source[:, index : index + 1]

        def pool_affine(target, source, factor, term):
            nc.gpsimd.tensor_scalar(out=target, in0=source, scalar1=factor, scalar2=term, op0=ALU.mult, op1=ALU.add)

        def row_sum(terms, bank, factor, other, total):
            nc.vector.scalar_tensor_tensor(
                out=terms[:], in0=bank[:], scalar=factor, in1=other[:], op0=ALU.mult, op1=ALU.mult, accum_out=total[:]
            )

        def keep_z1(g):
            nc.scalar.copy(z1[g][:], bank_a[g][:])

        def gate(g):
            nc.scalar.activation(
                out=th[g][:], in_=sum_mu[g][:], func=ACT.Tanh, scale=column(slope, g), bias=halves[:, g, 0:1]
            )

        def factors(g):
            half_og = halves[:, g, 1:2]
            for target, factor, term in ((a, half_og, half_og), (c, column(neg_slope, g), column(slope, g))):
                if g < POOL_FACTOR_GROUPS:
                    pool_affine(target[g][:], th[g][:], factor, term)
                else:
                    nc.scalar.activation(out=target[g][:], in_=th[g][:], func=ACT.Identity, scale=factor, bias=term)

        def add_base(g):
            nc.gpsimd.tensor_tensor(out=u_base[g][:], in0=u[g][:], in1=base_sb[:, g, :], op=ALU.add)

        def finish(g, cols):
            z1_source = z1[g] if g == LAST else bank_b[g]
            nc.vector.scalar_tensor_tensor(
                out=y[g][:, cols],
                in0=z1_source[:, cols],
                scalar=b[g][:],
                in1=u_base[g][:, cols],
                op0=ALU.mult,
                op1=ALU.add,
            )

        def finish_off_vector(g):
            b_z1 = tile("b_z1", [P, N], F32)
            nc.scalar.activation(out=b_z1[:], in_=z1[g][:], func=ACT.Copy, scale=b[g][:])
            nc.gpsimd.tensor_tensor(out=y[g][:], in0=b_z1[:], in1=u_base[g][:], op=ALU.add)

        def store(g, cols):
            nc.sync.dma_start(out=out[g][:, cols], in_=y[g][:, cols])

        pack(nc.vector.tensor_copy, dxq, dx_raw[0], 0, all_n)
        nc.vector.transpose(vecs[:], vec_rows[:])
        by_group = vecs[:].rearrange("p (g r) -> p g r", g=G)
        pool_affine(slope[:], by_group[:, :, 0], 0.5 / N, 0.0)
        pool_affine(halves[:], by_group[:, :, 1:3], 0.5, 0.0)
        pool_affine(neg_slope[:], by_group[:, :, 0], -0.5 / N, 0.0)
        keep_z1(0)
        pack(nc.vector.tensor_copy, dxq, dx_raw[1], PAIR, low_n)
        pack(nc.scalar.copy, dxq, dx_raw[1], PAIR, high_n)
        row_sum(terms_mu[0], bank_b[0], 1.0, z1[0], sum_mu[0])
        quantize(dxq, all_n)

        keep_z1(1)
        for g in range(POOL_FACTOR_GROUPS):
            keep_z1(g + 2)
            gate(g)
            factors(g)
            row_sum(terms_mu[g + 1], bank_b[g + 1], 1.0, z1[g + 1], sum_mu[g + 1])
        row_sum(terms_mu[LAST], bank_b[LAST], 1.0, z1[LAST], sum_mu[LAST])
        for g in range(G):
            product(bank_a[g], g, w1q, dxq)

        for step in range(G + FINISH_LAG):
            if step < G:
                g = step
                nc.scalar.activation(out=u[g][:], in_=bank_a[g][:], func=ACT.Copy, scale=a[g][:])
                product(bank_a[g], g, w2q, dxq)
                if g < LAST:
                    add_base(g)
                if POOL_FACTOR_GROUPS <= g + 1 < G:
                    factors(g + 1)
                if g + 2 < G:
                    gate(g + 2)
            if step >= FINISH_LAG:
                g = step - FINISH_LAG
                nc.scalar.activation(
                    out=b[g][:], in_=sum_t[g][:], func=ACT.Identity, scale=c[g][:], bias=sum_u[g][:]
                )
                if g == 0:
                    finish_off_vector(g)
                    store(g, all_n)
                    add_base(LAST)
                elif g == LAST:
                    for cols in (low_n, high_n):
                        finish(g, cols)
                        store(g, cols)
                else:
                    finish(g, all_n)
                    store(g, all_n)
            if step < G:
                g = step
                row_sum(terms_u[g], bank_b[g], c[g][:], u[g], sum_u[g])
                if 0 < g < LAST:
                    product(bank_b[g], g, w1q, xq)
            if 1 <= step <= G:
                g = step - 1
                row_sum(terms_t[g], bank_a[g], a[g][:], z1[g], sum_t[g])
